import numpy as np
import ml_dtypes


def mxq(x, axis, fmt="e4m3"):
    dtype, down = {"e4m3": (ml_dtypes.float8_e4m3fn, 7), "e5m2": (ml_dtypes.float8_e5m2, 14)}[fmt]
    v = np.moveaxis(np.asarray(x, np.float32).astype(ml_dtypes.bfloat16).astype(np.float64), axis, -1)
    blocks = v.reshape(v.shape[:-1] + (-1, 32))
    amax = np.abs(blocks).max(-1, keepdims=True)
    byte = np.maximum(np.where(amax > 0, np.frexp(amax)[1] - 1 + 127, 0) - down, 1)
    scale = np.exp2(byte - 127.0)
    codes = (blocks / scale).astype(np.float32).astype(dtype).astype(np.float64)
    return np.moveaxis((codes * scale).reshape(v.shape), -1, axis)


WIDE = False


def mx_kscale(k):
    if not WIDE:
        return np.ones(k)
    levels = np.array([10, -10, 5, -5, 0])
    if k % 512:
        return np.exp2(np.random.permutation(np.resize(levels, k // 32))).repeat(32)
    a = np.empty((k // 512, 16))
    for p in range(k // 512):
        a[p, :8] = np.random.permutation(np.resize(levels, 8))
        for g in range(8):
            far = levels[np.abs(levels - a[p, g]) >= 10]
            a[p, g + 8] = far[np.random.randint(len(far))]
    return np.exp2(a.ravel()).repeat(32)


def f64(x):
    return np.asarray(x).astype(np.float64)


def striped(idx):
    return np.tile(np.asarray(idx).reshape(-1, 16).T, (8, 1)).astype(np.uint16)


def unstriped(offs):
    return offs[:16].T.reshape(-1).astype(np.int64)


E2M1 = np.array([0.0, 0.5, 1.0, 1.5, 2.0, 3.0, 4.0, 6.0, -0.0, -0.5, -1.0, -1.5, -2.0, -3.0, -4.0, -6.0])


def pack_weight(w, fmt):
    k, n = w.shape
    w = f64(np.asarray(w, np.float32).astype(ml_dtypes.bfloat16)).reshape(k // 32, 32, n)
    amax = np.abs(w).max(1)
    if fmt == "e4m3":
        byte = np.frexp(amax)[1] - 1 + 127 - 7
    else:
        mant, ex = np.frexp(amax / 6.0)
        byte = np.where(mant > 0.5, ex, ex - 1) + 127
    byte = np.clip(np.where(amax > 0, byte, 1), 1, 254)
    scaled = (w * np.exp2(127.0 - byte)[:, None, :]).reshape(k, n).astype(np.float32)
    by_word = np.ascontiguousarray(scaled.reshape(k // 512, 128, 4, n).transpose(0, 1, 3, 2))
    if fmt == "e4m3":
        words = by_word.astype(ml_dtypes.float8_e4m3fn).view(np.uint8)
    else:
        c = by_word.astype(ml_dtypes.float4_e2m1fn).view(np.uint8) & 0xF
        words = (c[..., 0::2] | (c[..., 1::2] << 4)).reshape(k // 512, 128, 2 * n)
    return np.ascontiguousarray(words), np.ascontiguousarray(byte.astype(np.uint8).reshape(k // 512, 16, n))


def unpack_weight(words, scales, fmt):
    g, _, n = scales.shape
    words = np.ascontiguousarray(words).reshape(g, 128, n, -1)
    if fmt == "e4m3":
        vals = words.view(ml_dtypes.float8_e4m3fn).astype(np.float64)
    else:
        nib = np.empty((g, 128, n, 4), np.uint8)
        nib[..., 0::2] = words & 0xF
        nib[..., 1::2] = words >> 4
        vals = E2M1[nib]
    vals = vals * np.repeat(np.exp2(scales.astype(np.float64) - 127.0), 8, axis=1)[..., None]
    return vals.transpose(0, 1, 3, 2).reshape(g * 512, n)


def bf(x):
    return np.asarray(x, np.float32).astype(ml_dtypes.bfloat16)


def planes(Y):
    r, m = Y.shape
    b = f64(bf(Y)).reshape(r // 32, 32, m)
    amax = np.abs(b).max(1)
    byte = np.clip(np.where(amax > 0, np.frexp(amax)[1] - 1 + 127 - 7, 1), 1, 254)
    codes = (b * np.exp2(127.0 - byte)[:, None, :]).reshape(r, m).astype(np.float32).astype(ml_dtypes.float8_e4m3fn).view(np.uint8)
    words = codes.reshape(r // 512, 128, 4, m).transpose(0, 1, 3, 2)
    return np.ascontiguousarray(words), np.ascontiguousarray(byte.astype(np.uint8).reshape(r // 512, 16, m))


D, T, I, J, U, Z, E = 512, 2048, 512, 512, 1024, 1024, 512


def setup_inputs():
    n = np.random.standard_normal
    idx = np.random.permutation(T)[:I]
    idx2 = np.random.permutation(U)[:J]
    idx3 = np.random.permutation(Z)[:J]
    fd = mx_kscale(D)
    fi = mx_kscale(I)
    ti = np.ones(T)
    ti[idx] = fi
    keysp = pack_weight(n((D, T)) / fd[:, None], "e2m1")
    return {
        "keys_words": keysp[0],
        "keys_scales": keysp[1],
        "notes": (n((D, U)) * 1.0 / np.sqrt(D) * fd[:, None]).astype(np.float32),
        "users2": (n((D, Z)) * 1.0 / np.sqrt(D) * fd[:, None]).astype(np.float32),
        "rowf": (np.random.uniform(0.02, 0.08, (I, 1)) * fi[:, None]).astype(np.float32),
        "vals": (n((E, T)) / ti).astype(np.float32),
        "mem": (np.random.uniform(0.3, 1.0, (1, J))).astype(np.float32),
        "offs": striped(idx),
        "offs2": striped(idx2),
        "offs3": striped(idx3),
    }


def reference(keys_words, keys_scales, notes, users2, rowf, vals, mem, offs, offs2, offs3):
    idx = unstriped(offs)
    idx2 = unstriped(offs2)
    idx3 = unstriped(offs3)
    keysu = unpack_weight(keys_words, keys_scales, "e2m1")
    keysidxg = keysu[:, idx]
    notesq = mxq(f64(notes), 0, "e4m3")
    g1 = keysidxg.T @ notesq
    users2idx3q = mxq(f64(users2)[:, idx3], 0, "e4m3")
    g2 = keysidxg.T @ users2idx3q
    g0 = np.maximum(g1[:, idx2], g2)
    gr1 = g0 * f64(rowf)
    vt1 = f64(vals)[:, idx].T
    vt1q = mxq(vt1, 0, "e4m3")
    gr1q = mxq(gr1, 0, "e4m3")
    o = vt1q.T @ gr1q
    o1 = np.pad(o, ((0, 0), (1, 0)))[:, :J]
    y = o - o1 * f64(mem)
    words, scales = planes(y)
    return y, words, scales

@@ -1,0 +1,247 @@
+from contextlib import ExitStack
+
+import concourse.mybir as mybir
+from concourse.masks import make_identity
+
+D, T, I, J, U, Z, E = 512, 2048, 512, 512, 1024, 1024, 512
+FLOPS = 2 * D * I * U + 2 * D * I * J + 2 * I * E * J
+
+F32 = mybir.dt.float32
+BF16 = mybir.dt.bfloat16
+I32 = mybir.dt.int32
+U32 = mybir.dt.uint32
+U16 = mybir.dt.uint16
+U8 = mybir.dt.uint8
+FP8X4 = mybir.dt.float8_e4m3fn_x4
+FP4X4 = mybir.dt.float4_e2m1fn_x4
+ALU = mybir.AluOpType
+COPY = mybir.ActivationFunctionType.Copy
+
+P = 128
+PACK = 4
+BANK = 512
+HALF = J // 2
+
+
+def weave(engine_copy, woven, planes):
+    engine_copy(
+        out=woven.rearrange("p (c i) t -> p c t i", i=4),
+        in_=planes.rearrange("p t (c i) -> p c t i", i=4),
+    )
+
+
+def shared_weave(nc, woven, planes, scalar_cols):
+    weave(nc.scalar.copy, woven[:, :scalar_cols, :], planes[:, :, :scalar_cols])
+    weave(nc.vector.tensor_copy, woven[:, scalar_cols:, :], planes[:, :, scalar_cols:])
+
+
+def quantize(nc, codes, scales, woven):
+    nc.vector.quantize_mx(out=codes.bitcast(FP8X4), scales=scales, in_=woven.rearrange("p c t -> p (c t)"))
+
+
+def tile_attend_tab_wideandown_changes_pl_kernel(
+    tc, keys_words, keys_scales, notes, users2, rowf, vals, mem, offs, offs2, offs3, out_0, out_1, out_2
+):
+    nc = tc.nc
+    with ExitStack() as ctx:
+        lists = ctx.enter_context(tc.tile_pool(name="lists", bufs=1))
+        sb = ctx.enter_context(tc.tile_pool(name="sb", bufs=1))
+        psum = ctx.enter_context(tc.psum_pool(name="psum", bufs=1))
+
+        token_list = lists.tile([P, I // 16], U16, name="token_list")
+        note_list = lists.tile([P, J // 16], U16, name="note_list")
+        user_list = lists.tile([P, J // 16], U16, name="user_list")
+
+        key_words = sb.tile([P, T], U16, name="key_words")
+        key_scales = sb.tile([P, T], U8, name="key_scales")
+        note_rows = [sb.tile([P, PACK, BANK], F32, name=f"note_rows{h}") for h in range(U // BANK)]
+        user_rows = [sb.tile([P, Z], F32, name=f"user_rows{t}") for t in range(PACK)]
+        val_rows = [
+            sb.tile([P, T], F32, name=f"val_rows{t}", tag=f"val_rows{t}", align_bytes=64) for t in range(PACK)
+        ]
+        row_factor = sb.tile([P, PACK], F32, name="row_factor")
+        mem_cols = sb.tile([P, PACK], F32, name="mem_cols")
+
+        nc.gpsimd.memset(key_scales[:].bitcast(I32), 0)
+        notes_v = notes.rearrange("(p t) u -> p t u", t=PACK)
+        users_v = users2.rearrange("(p t) z -> p t z", t=PACK)
+        vals_v = vals.rearrange("(p t) c -> p t c", t=PACK)
+        nc.sync.dma_start(token_list[:], offs)
+        nc.sync.dma_start(out=key_words[:].bitcast(I32), in_=keys_words[0].bitcast(I32))
+        for q in range(4):
+            nc.sync.dma_start(
+                out=key_scales[32 * q : 32 * q + 4, :].bitcast(I32),
+                in_=keys_scales[0, 4 * q : 4 * q + 4, :].bitcast(I32),
+            )
+        for h in range(U // BANK):
+            nc.sync.dma_start(out=note_rows[h][:], in_=notes_v[:, :, h * BANK : (h + 1) * BANK])
+            if h == 0:
+                nc.sync.dma_start(out=mem_cols[:], in_=mem.rearrange("o (p c) -> p (o c)", c=PACK))
+        nc.sync.dma_start(user_list[:], offs3)
+        nc.sync.dma_start(note_list[:], offs2)
+        nc.sync.dma_start(out=row_factor[:], in_=rowf.rearrange("(p t) o -> p (t o)", t=PACK))
+        for t in range(PACK):
+            nc.sync.dma_start(out=user_rows[t][:], in_=users_v[:, t, :])
+        for t in range(PACK):
+            nc.sync.dma_start(out=val_rows[t][:], in_=vals_v[:, t, :])
+
+        ident = sb.tile([P, P], F32, name="ident")
+        make_identity(nc, ident[:])
+
+        y = sb.tile([P, PACK, J], F32, name="y")
+        nc.vector.memset(y[:, :, 0:1], 0.0)
+
+        picked_words = sb.tile([P, I], U16, name="picked_words")
+        dealt_words = sb.tile([P, I], U16, name="dealt_words", align_bytes=64)
+        dealt_scales = sb.tile([P, I], U8, name="dealt_scales", align_bytes=64)
+        nc.vector.tensor_copy(picked_words[:], key_words[:].indirect(token_list[:]))
+        nc.vector.tensor_copy(
+            out=dealt_words[:].rearrange("p (r s) -> p r s", r=PACK),
+            in_=picked_words[:].rearrange("p (s r) -> p r s", r=PACK),
+        )
+        nc.vector.tensor_copy(
+            dealt_scales[:].rearrange("p (r s) -> p s r", r=PACK), key_scales[:].indirect(token_list[:])
+        )
+
+
+        def keys_times(bank, r, codes, scales):
+            cols = slice(r * P, (r + 1) * P)
+            nc.tensor.matmul_mx(
+                out=bank,
+                lhsT=dealt_words[:, cols].bitcast(FP4X4),
+                lhsT_scale=dealt_scales[:, cols],
+                rhs=codes.bitcast(FP8X4),
+                rhs_scale=scales,
+                start=True,
+                stop=True,
+            )
+
+        mem_turned = psum.tile([P, PACK, P], F32, name="mem_turned", tag="narrow0")
+        for c in range(PACK):
+            nc.tensor.transpose(mem_turned[:, c, :], mem_cols[:, c : c + 1].to_broadcast([P, P]), ident[:])
+        mem_row = sb.tile([P, J], F32, name="mem_row")
+        nc.scalar.copy(
+            out=mem_row[:].rearrange("p (k c) -> p k c", c=PACK), in_=mem_turned[:].rearrange("p c k -> p k c")
+        )
+
+        wide = [sb.tile([P, U], F32, name=f"wide{r}") for r in range(PACK)]
+        for h in range(U // BANK):
+            note_woven = sb.tile([P, BANK, PACK], BF16, name=f"note_woven{h}", align_bytes=64)
+            note_codes = sb.tile([P, BANK], U32, name=f"note_codes{h}", align_bytes=64)
+            note_scales = sb.tile([P, BANK], U8, name=f"note_scales{h}", align_bytes=64)
+            if h == 0:
+                shared_weave(nc, note_woven, note_rows[h], 192)
+            else:
+                weave(nc.vector.tensor_copy, note_woven[:], note_rows[h][:])
+            quantize(nc, note_codes[:], note_scales[:], note_woven[:])
+            for r in range(PACK):
+                bank = psum.tile([P, BANK], F32, name="wide_bank", tag=f"main{r}")
+                keys_times(bank[:], r, note_codes[:], note_scales[:])
+                nc.scalar.copy(out=wide[r][:, h * BANK : (h + 1) * BANK], in_=bank[:])
+
+        halves = [slice(h * HALF, (h + 1) * HALF) for h in range(2)]
+        list_halves = [slice(h * HALF // 16, (h + 1) * HALF // 16) for h in range(2)]
+        user_picked = [sb.tile([P, PACK, HALF], BF16, name=f"user_picked{h}") for h in range(2)]
+        wide_picked = [sb.tile([P, PACK, HALF], F32, name=f"wide_picked{h}") for h in range(2)]
+        for h in range(2):
+            for r in range(PACK):
+                nc.scalar.activation(wide_picked[h][:, r, :], wide[r][:].indirect(note_list[:, list_halves[h]]), COPY)
+        def pick_users(t, h):
+            nc.vector.tensor_copy(user_picked[h][:, t, :], user_rows[t][:].indirect(user_list[:, list_halves[h]]))
+
+        for t in range(PACK - 1):
+            for h in range(2):
+                pick_users(t, h)
+        user_codes, user_scales = [], []
+        for h in range(2):
+            pick_users(PACK - 1, h)
+            user_woven = sb.tile([P, HALF, PACK], BF16, name=f"user_woven{h}", align_bytes=64)
+            user_codes.append(sb.tile([P, HALF], U32, name=f"user_codes{h}", align_bytes=64))
+            user_scales.append(sb.tile([P, HALF], U8, name=f"user_scales{h}", align_bytes=64))
+            weave(nc.vector.tensor_copy, user_woven[:], user_picked[h][:])
+            quantize(nc, user_codes[h][:], user_scales[h][:], user_woven[:])
+
+        table_codes = sb.tile([P, J], U32, name="table_codes", align_bytes=64)
+        table_scales = sb.tile([P, J], U8, name="table_scales", align_bytes=64)
+        for h in range(2):
+            table = sb.tile([P, PACK, HALF], BF16, name=f"table{h}")
+            for pair in range(2):
+                narrow = psum.tile([P, 2, HALF], F32, name="narrow", tag=f"narrow{2 * h + pair}")
+                for k in range(2):
+                    keys_times(narrow[:, k, :], 2 * pair + k, user_codes[h][:], user_scales[h][:])
+                larger = sb.tile([P, 2, HALF], F32, name=f"larger{h}{pair}")
+                nc.vector.tensor_tensor(
+                    out=larger[:], in0=narrow[:], in1=wide_picked[h][:, 2 * pair : 2 * pair + 2, :], op=ALU.max
+                )
+                engine = nc.vector if (h, pair) == (1, 1) else nc.gpsimd
+                for k in range(2):
+                    r = 2 * pair + k
+                    engine.tensor_scalar(
+                        out=table[:, r, :],
+                        in0=larger[:, k, :],
+                        scalar1=row_factor[:, r : r + 1],
+                        scalar2=1.0,
+                        op0=ALU.mult,
+                        op1=ALU.mult,
+                    )
+            table_woven = sb.tile([P, HALF, PACK], BF16, name=f"table_woven{h}", tag=f"table_woven{h}", align_bytes=64)
+            weave(nc.vector.tensor_copy, table_woven[:], table[:])
+            quantize(nc, table_codes[:, halves[h]], table_scales[:, halves[h]], table_woven[:])
+
+        out_v = out_0.rearrange("(p t) c -> p t c", t=PACK)
+        groups = [(0, 1), (2,), (3,)]
+        val_codes, val_scales = {}, {}
+        turned = []
+        for t in range(PACK):
+            val_picked = sb.tile([P, I], BF16, name=f"val_picked{t}")
+            nc.scalar.activation(val_picked[:], val_rows[t][:].indirect(token_list[:]), COPY)
+            pairs = val_picked[:].bitcast(F32)
+            turned.append(psum.tile([P, 2, P], F32, name="turned", tag=f"main{t}"))
+            for u in range(2):
+                nc.tensor.transpose(turned[t][:, u, :], pairs[:, u : I // 2 : 2], ident[:])
+        for group in groups:
+            width = len(group) * P
+            woven_tag = f"val_rows{group[-1] + 1}" if group[-1] + 1 < PACK else "val_woven_last"
+            val_woven = sb.tile([P, width, PACK], BF16, name=f"val_woven{group[0]}", tag=woven_tag, align_bytes=64)
+            for k, t in enumerate(group):
+                nc.scalar.copy(
+                    out=val_woven[:, k * P : (k + 1) * P, :].bitcast(F32), in_=turned[t][:].rearrange("p u e -> p e u")
+                )
+            tag = "table_woven1" if group[0] == 0 else f"val_codes{group[0]}"
+            codes = sb.tile([P, width], U32, name=f"val_codes{group[0]}", tag=tag, align_bytes=64)
+            scales = sb.tile([P, width], U8, name=f"val_scales{group[0]}", align_bytes=64)
+            quantize(nc, codes[:], scales[:], val_woven[:])
+            for k, t in enumerate(group):
+                val_codes[t] = codes[:, k * P : (k + 1) * P]
+                val_scales[t] = scales[:, k * P : (k + 1) * P]
+
+        for pair in range(2):
+            sums = {}
+            for t in (2 * pair, 2 * pair + 1):
+                sums[t] = psum.tile([P, BANK], F32, name="sums", tag=f"main{t ^ 1}")
+                nc.tensor.matmul_mx(
+                    out=sums[t][:],
+                    lhsT=val_codes[t].bitcast(FP8X4),
+                    lhsT_scale=val_scales[t],
+                    rhs=table_codes[:].bitcast(FP8X4),
+                    rhs_scale=table_scales[:],
+                    start=True,
+                    stop=True,
+                )
+            for t in sums:
+                nc.vector.tensor_tensor(out=y[:, t, 1:J], in0=sums[t][:, 0 : J - 1], in1=mem_row[:, 1:J], op=ALU.mult)
+            for t in sums:
+                nc.vector.tensor_tensor(out=y[:, t, :], in0=sums[t][:], in1=y[:, t, :], op=ALU.subtract)
+                nc.sync.dma_start(out=out_v[:, t, :], in_=y[:, t, :])
+
+        y_woven = sb.tile([P, J, PACK], BF16, name="y_woven", align_bytes=64)
+        y_codes = sb.tile([P, J], U32, name="y_codes", align_bytes=64)
+        y_scales = sb.tile([P, J], U8, name="y_scales", align_bytes=64)
+        shared_weave(nc, y_woven, y, 160)
+        quantize(nc, y_codes[:], y_scales[:], y_woven[:])
+        nc.sync.dma_start(out=out_1[0].rearrange("p c t -> p (c t)").bitcast(I32), in_=y_codes[:].bitcast(I32))
+        for q in range(4):
+            queue = nc.sync if q % 2 else nc.scalar
+            queue.dma_start(
+                out=out_2[0, 4 * q : 4 * q + 4, :].bitcast(I32), in_=y_scales[32 * q : 32 * q + 4, :].bitcast(I32)
+            )

@@ -21,6 +21,9 @@ P = 128
 PACK = 4
 BANK = 512
 HALF = J // 2
+CHUNK = 256
+SCALAR_CHUNKS = 2
+SCALAR_COLS = 192
 
 
 def weave(engine_copy, woven, planes):
@@ -28,11 +31,6 @@ def weave(engine_copy, woven, planes):
         out=woven.rearrange("p (c i) t -> p c t i", i=4),
         in_=planes.rearrange("p t (c i) -> p c t i", i=4),
     )
-
-
-def shared_weave(nc, woven, planes, scalar_cols):
-    weave(nc.scalar.copy, woven[:, :scalar_cols, :], planes[:, :, :scalar_cols])
-    weave(nc.vector.tensor_copy, woven[:, scalar_cols:, :], planes[:, :, scalar_cols:])
 
 
 def quantize(nc, codes, scales, woven):
@@ -52,12 +50,12 @@ def tile_attend_tab_wideandown_changes_pl_kernel(
         note_list = lists.tile([P, J // 16], U16, name="note_list")
         user_list = lists.tile([P, J // 16], U16, name="user_list")
 
-        key_words = sb.tile([P, T], U16, name="key_words")
-        key_scales = sb.tile([P, T], U8, name="key_scales")
-        note_rows = [sb.tile([P, PACK, BANK], F32, name=f"note_rows{h}") for h in range(U // BANK)]
-        user_rows = [sb.tile([P, Z], F32, name=f"user_rows{t}") for t in range(PACK)]
+        key_words = sb.tile([P, T], U16, name="key_words", align_bytes=256)
+        key_scales = sb.tile([P, T], U8, name="key_scales", align_bytes=256)
+        note_rows = [sb.tile([P, PACK, CHUNK], F32, name=f"note_rows{c}", align_bytes=256) for c in range(U // CHUNK)]
+        user_rows = [sb.tile([P, Z], F32, name=f"user_rows{t}", align_bytes=256) for t in range(PACK)]
         val_rows = [
-            sb.tile([P, T], F32, name=f"val_rows{t}", tag=f"val_rows{t}", align_bytes=64) for t in range(PACK)
+            sb.tile([P, T], F32, name=f"val_rows{t}", tag=f"val_rows{t}", align_bytes=256) for t in range(PACK)
         ]
         row_factor = sb.tile([P, PACK], F32, name="row_factor")
         mem_cols = sb.tile([P, PACK], F32, name="mem_cols")
@@ -66,16 +64,16 @@ def tile_attend_tab_wideandown_changes_pl_kernel(
         notes_v = notes.rearrange("(p t) u -> p t u", t=PACK)
         users_v = users2.rearrange("(p t) z -> p t z", t=PACK)
         vals_v = vals.rearrange("(p t) c -> p t c", t=PACK)
-        nc.sync.dma_start(token_list[:], offs)
         nc.sync.dma_start(out=key_words[:].bitcast(I32), in_=keys_words[0].bitcast(I32))
+        nc.sync.dma_start(token_list[:], offs)
         for q in range(4):
             nc.sync.dma_start(
                 out=key_scales[32 * q : 32 * q + 4, :].bitcast(I32),
                 in_=keys_scales[0, 4 * q : 4 * q + 4, :].bitcast(I32),
             )
-        for h in range(U // BANK):
-            nc.sync.dma_start(out=note_rows[h][:], in_=notes_v[:, :, h * BANK : (h + 1) * BANK])
-            if h == 0:
+        for c in range(U // CHUNK):
+            nc.sync.dma_start(out=note_rows[c][:], in_=notes_v[:, :, c * CHUNK : (c + 1) * CHUNK])
+            if c == 1:
                 nc.sync.dma_start(out=mem_cols[:], in_=mem.rearrange("o (p c) -> p (o c)", c=PACK))
         nc.sync.dma_start(user_list[:], offs3)
         nc.sync.dma_start(note_list[:], offs2)
@@ -88,21 +86,20 @@ def tile_attend_tab_wideandown_changes_pl_kernel(
         ident = sb.tile([P, P], F32, name="ident")
         make_identity(nc, ident[:])
 
-        y = sb.tile([P, PACK, J], F32, name="y")
-        nc.vector.memset(y[:, :, 0:1], 0.0)
+        carried = sb.tile([P, PACK, J], F32, name="carried")
+        nc.vector.memset(carried[:, :, 0:1], 0.0)
 
         picked_words = sb.tile([P, I], U16, name="picked_words")
         dealt_words = sb.tile([P, I], U16, name="dealt_words", align_bytes=64)
         dealt_scales = sb.tile([P, I], U8, name="dealt_scales", align_bytes=64)
         nc.vector.tensor_copy(picked_words[:], key_words[:].indirect(token_list[:]))
         nc.vector.tensor_copy(
+            dealt_scales[:].rearrange("p (r s) -> p s r", r=PACK), key_scales[:].indirect(token_list[:])
+        )
+        nc.vector.tensor_copy(
             out=dealt_words[:].rearrange("p (r s) -> p r s", r=PACK),
             in_=picked_words[:].rearrange("p (s r) -> p r s", r=PACK),
         )
-        nc.vector.tensor_copy(
-            dealt_scales[:].rearrange("p (r s) -> p s r", r=PACK), key_scales[:].indirect(token_list[:])
-        )
-
 
         def keys_times(bank, r, codes, scales):
             cols = slice(r * P, (r + 1) * P)
@@ -116,6 +113,12 @@ def tile_attend_tab_wideandown_changes_pl_kernel(
                 stop=True,
             )
 
+        note_woven = [
+            sb.tile([P, CHUNK, PACK], BF16, name=f"note_woven{c}", align_bytes=64) for c in range(U // CHUNK)
+        ]
+        for c in range(SCALAR_CHUNKS):
+            weave(nc.scalar.copy, note_woven[c][:], note_rows[c][:])
+
         mem_turned = psum.tile([P, PACK, P], F32, name="mem_turned", tag="narrow0")
         for c in range(PACK):
             nc.tensor.transpose(mem_turned[:, c, :], mem_cols[:, c : c + 1].to_broadcast([P, P]), ident[:])
@@ -124,122 +127,165 @@ def tile_attend_tab_wideandown_changes_pl_kernel(
             out=mem_row[:].rearrange("p (k c) -> p k c", c=PACK), in_=mem_turned[:].rearrange("p c k -> p k c")
         )
 
-        wide = [sb.tile([P, U], F32, name=f"wide{r}") for r in range(PACK)]
-        for h in range(U // BANK):
-            note_woven = sb.tile([P, BANK, PACK], BF16, name=f"note_woven{h}", align_bytes=64)
-            note_codes = sb.tile([P, BANK], U32, name=f"note_codes{h}", align_bytes=64)
-            note_scales = sb.tile([P, BANK], U8, name=f"note_scales{h}", align_bytes=64)
-            if h == 0:
-                shared_weave(nc, note_woven, note_rows[h], 192)
-            else:
-                weave(nc.vector.tensor_copy, note_woven[:], note_rows[h][:])
-            quantize(nc, note_codes[:], note_scales[:], note_woven[:])
-            for r in range(PACK):
-                bank = psum.tile([P, BANK], F32, name="wide_bank", tag=f"main{r}")
-                keys_times(bank[:], r, note_codes[:], note_scales[:])
-                nc.scalar.copy(out=wide[r][:, h * BANK : (h + 1) * BANK], in_=bank[:])
+        wide = sb.tile([P, PACK, U], F32, name="wide")
+        for c in range(U // CHUNK):
+            note_codes = sb.tile([P, CHUNK], U32, name=f"note_codes{c}", align_bytes=64)
+            note_scales = sb.tile([P, CHUNK], U8, name=f"note_scales{c}", align_bytes=64)
+            if c >= SCALAR_CHUNKS:
+                weave(nc.vector.tensor_copy, note_woven[c][:], note_rows[c][:])
+            quantize(nc, note_codes[:], note_scales[:], note_woven[c][:])
+            for pair in range(2):
+                bank = psum.tile([P, 2, CHUNK], F32, name="wide_bank", tag=f"main{(2 * c + pair) % 4}")
+                for k in range(2):
+                    keys_times(bank[:, k, :], 2 * pair + k, note_codes[:], note_scales[:])
+                nc.scalar.copy(out=wide[:, 2 * pair : 2 * pair + 2, c * CHUNK : (c + 1) * CHUNK], in_=bank[:])
 
         halves = [slice(h * HALF, (h + 1) * HALF) for h in range(2)]
         list_halves = [slice(h * HALF // 16, (h + 1) * HALF // 16) for h in range(2)]
-        user_picked = [sb.tile([P, PACK, HALF], BF16, name=f"user_picked{h}") for h in range(2)]
-        wide_picked = [sb.tile([P, PACK, HALF], F32, name=f"wide_picked{h}") for h in range(2)]
-        for h in range(2):
-            for r in range(PACK):
-                nc.scalar.activation(wide_picked[h][:, r, :], wide[r][:].indirect(note_list[:, list_halves[h]]), COPY)
-        def pick_users(t, h):
-            nc.vector.tensor_copy(user_picked[h][:, t, :], user_rows[t][:].indirect(user_list[:, list_halves[h]]))
+        last = PACK - 1
+        wide_picked = [sb.tile([P, 2, J], F32, name=f"wide_picked{pair}") for pair in range(2)]
+        for r in range(PACK):
+            nc.scalar.activation(wide_picked[r // 2][:, r % 2, :], wide[:, r, :].indirect(note_list[:]), COPY)
 
-        for t in range(PACK - 1):
-            for h in range(2):
-                pick_users(t, h)
-        user_codes, user_scales = [], []
+        user_picked = sb.tile([P, PACK, J], BF16, name="user_picked")
+        for t in range(last):
+            nc.vector.tensor_copy(user_picked[:, t, :], user_rows[t][:].indirect(user_list[:]))
         for h in range(2):
-            pick_users(PACK - 1, h)
-            user_woven = sb.tile([P, HALF, PACK], BF16, name=f"user_woven{h}", align_bytes=64)
-            user_codes.append(sb.tile([P, HALF], U32, name=f"user_codes{h}", align_bytes=64))
-            user_scales.append(sb.tile([P, HALF], U8, name=f"user_scales{h}", align_bytes=64))
-            weave(nc.vector.tensor_copy, user_woven[:], user_picked[h][:])
-            quantize(nc, user_codes[h][:], user_scales[h][:], user_woven[:])
+            nc.vector.tensor_copy(
+                user_picked[:, last, halves[h]], user_rows[last][:].indirect(user_list[:, list_halves[h]])
+            )
+        user_woven = [sb.tile([P, HALF, PACK], BF16, name=f"user_woven{h}", align_bytes=64) for h in range(2)]
+        user_codes = [sb.tile([P, HALF], U32, name=f"user_codes{h}", align_bytes=64) for h in range(2)]
+        user_scales = [sb.tile([P, HALF], U8, name=f"user_scales{h}", align_bytes=64) for h in range(2)]
+        for h in range(2):
+            weave(nc.vector.tensor_copy, user_woven[h][:], user_picked[:, :, halves[h]])
+        for h in range(2):
+            quantize(nc, user_codes[h][:], user_scales[h][:], user_woven[h][:])
 
+        table = sb.tile([P, PACK, J], BF16, name="table")
+        blocks = [(pair, h) for pair in range(2) for h in range(2)]
+        larger = [
+            sb.tile([P, 2, HALF], F32, name=f"larger{b}", tag=f"larger{b}", align_bytes=64) for b in range(len(blocks))
+        ]
+
+        def take_larger(b):
+            pair, h = blocks[b]
+            narrow = psum.tile([P, 2, HALF], F32, name="narrow", tag=f"narrow{b}")
+            for k in range(2):
+                keys_times(narrow[:, k, :], 2 * pair + k, user_codes[h][:], user_scales[h][:])
+            nc.vector.tensor_tensor(out=larger[b][:], in0=narrow[:], in1=wide_picked[pair][:, :, halves[h]], op=ALU.max)
+
+        def scale_rows(b):
+            pair, h = blocks[b]
+            for k in range(2):
+                r = 2 * pair + k
+                nc.vector.tensor_scalar(
+                    out=table[:, r, halves[h]],
+                    in0=larger[b][:, k, :],
+                    scalar1=row_factor[:, r : r + 1],
+                    scalar2=None,
+                    op0=ALU.mult,
+                )
+
+        take_larger(0)
+        for b in range(1, len(blocks)):
+            take_larger(b)
+            scale_rows(b - 1)
+        scale_rows(len(blocks) - 1)
+
+        table_woven = [
+            sb.tile([P, HALF, PACK], BF16, name=f"table_woven{h}", tag=f"table_woven{h}", align_bytes=64)
+            for h in range(2)
+        ]
         table_codes = sb.tile([P, J], U32, name="table_codes", align_bytes=64)
         table_scales = sb.tile([P, J], U8, name="table_scales", align_bytes=64)
-        for h in range(2):
-            table = sb.tile([P, PACK, HALF], BF16, name=f"table{h}")
-            for pair in range(2):
-                narrow = psum.tile([P, 2, HALF], F32, name="narrow", tag=f"narrow{2 * h + pair}")
-                for k in range(2):
-                    keys_times(narrow[:, k, :], 2 * pair + k, user_codes[h][:], user_scales[h][:])
-                larger = sb.tile([P, 2, HALF], F32, name=f"larger{h}{pair}")
-                nc.vector.tensor_tensor(
-                    out=larger[:], in0=narrow[:], in1=wide_picked[h][:, 2 * pair : 2 * pair + 2, :], op=ALU.max
-                )
-                engine = nc.vector if (h, pair) == (1, 1) else nc.gpsimd
-                for k in range(2):
-                    r = 2 * pair + k
-                    engine.tensor_scalar(
-                        out=table[:, r, :],
-                        in0=larger[:, k, :],
-                        scalar1=row_factor[:, r : r + 1],
-                        scalar2=1.0,
-                        op0=ALU.mult,
-                        op1=ALU.mult,
-                    )
-            table_woven = sb.tile([P, HALF, PACK], BF16, name=f"table_woven{h}", tag=f"table_woven{h}", align_bytes=64)
-            weave(nc.vector.tensor_copy, table_woven[:], table[:])
-            quantize(nc, table_codes[:, halves[h]], table_scales[:, halves[h]], table_woven[:])
 
-        out_v = out_0.rearrange("(p t) c -> p t c", t=PACK)
-        groups = [(0, 1), (2,), (3,)]
-        val_codes, val_scales = {}, {}
-        turned = []
-        for t in range(PACK):
-            val_picked = sb.tile([P, I], BF16, name=f"val_picked{t}")
+        def turn_values(t, picked_tag):
+            val_picked = sb.tile([P, I], BF16, name=f"val_picked{t}", tag=picked_tag, align_bytes=64)
             nc.scalar.activation(val_picked[:], val_rows[t][:].indirect(token_list[:]), COPY)
             pairs = val_picked[:].bitcast(F32)
-            turned.append(psum.tile([P, 2, P], F32, name="turned", tag=f"main{t}"))
+            turned = psum.tile([P, 2, P], F32, name="turned", tag=f"main{t}")
             for u in range(2):
-                nc.tensor.transpose(turned[t][:, u, :], pairs[:, u : I // 2 : 2], ident[:])
-        for group in groups:
-            width = len(group) * P
-            woven_tag = f"val_rows{group[-1] + 1}" if group[-1] + 1 < PACK else "val_woven_last"
-            val_woven = sb.tile([P, width, PACK], BF16, name=f"val_woven{group[0]}", tag=woven_tag, align_bytes=64)
-            for k, t in enumerate(group):
-                nc.scalar.copy(
-                    out=val_woven[:, k * P : (k + 1) * P, :].bitcast(F32), in_=turned[t][:].rearrange("p u e -> p e u")
-                )
-            tag = "table_woven1" if group[0] == 0 else f"val_codes{group[0]}"
-            codes = sb.tile([P, width], U32, name=f"val_codes{group[0]}", tag=tag, align_bytes=64)
-            scales = sb.tile([P, width], U8, name=f"val_scales{group[0]}", align_bytes=64)
-            quantize(nc, codes[:], scales[:], val_woven[:])
-            for k, t in enumerate(group):
-                val_codes[t] = codes[:, k * P : (k + 1) * P]
-                val_scales[t] = scales[:, k * P : (k + 1) * P]
+                nc.tensor.transpose(turned[:, u, :], pairs[:, u : I // 2 : 2], ident[:])
+            return turned[:].rearrange("p u e -> p e u")
 
-        for pair in range(2):
-            sums = {}
-            for t in (2 * pair, 2 * pair + 1):
-                sums[t] = psum.tile([P, BANK], F32, name="sums", tag=f"main{t ^ 1}")
+        def value_operands(pair, picked_tags, codes_tag):
+            turned = [turn_values(2 * pair + k, picked_tags[k]) for k in range(2)]
+            woven = sb.tile(
+                [P, 2 * P, PACK], BF16, name=f"val_woven{pair}", tag=f"val_rows{2 * pair + 1}", align_bytes=256
+            )
+            codes = sb.tile([P, 2 * P], U32, name=f"val_codes{pair}", tag=codes_tag, align_bytes=64)
+            scales = sb.tile([P, 2 * P], U8, name=f"val_scales{pair}", align_bytes=64)
+            for k in range(2):
+                nc.scalar.copy(out=woven[:, k * P : (k + 1) * P, :].bitcast(F32), in_=turned[k])
+            quantize(nc, codes[:], scales[:], woven[:])
+            return codes, scales
+
+        def values_times_table(pair, h, codes, scales):
+            sums = psum.tile([P, 2, HALF], F32, name="sums", tag=f"narrow{2 * pair + h}")
+            for k in range(2):
+                plane = slice(k * P, (k + 1) * P)
                 nc.tensor.matmul_mx(
-                    out=sums[t][:],
-                    lhsT=val_codes[t].bitcast(FP8X4),
-                    lhsT_scale=val_scales[t],
-                    rhs=table_codes[:].bitcast(FP8X4),
-                    rhs_scale=table_scales[:],
+                    out=sums[:, k, :],
+                    lhsT=codes[:, plane].bitcast(FP8X4),
+                    lhsT_scale=scales[:, plane],
+                    rhs=table_codes[:, halves[h]].bitcast(FP8X4),
+                    rhs_scale=table_scales[:, halves[h]],
                     start=True,
                     stop=True,
                 )
-            for t in sums:
-                nc.vector.tensor_tensor(out=y[:, t, 1:J], in0=sums[t][:, 0 : J - 1], in1=mem_row[:, 1:J], op=ALU.mult)
-            for t in sums:
-                nc.vector.tensor_tensor(out=y[:, t, :], in0=sums[t][:], in1=y[:, t, :], op=ALU.subtract)
-                nc.sync.dma_start(out=out_v[:, t, :], in_=y[:, t, :])
+            return sums
 
-        y_woven = sb.tile([P, J, PACK], BF16, name="y_woven", align_bytes=64)
+        y = sb.tile([P, PACK, J], F32, name="y", align_bytes=256)
+        out_v = out_0.rearrange("(p t) c -> p t c", t=PACK)
+
+        def times_mem(pair, h, sums):
+            first = h * HALF + 1
+            width = min(HALF, J - first)
+            nc.vector.tensor_tensor(
+                out=carried[:, 2 * pair : 2 * pair + 2, first : first + width],
+                in0=sums[:, :, 0:width],
+                in1=mem_row[:, first : first + width].unsqueeze(1).to_broadcast([P, 2, width]),
+                op=ALU.mult,
+            )
+
+        def less_carried(pair, h, sums):
+            planes = slice(2 * pair, 2 * pair + 2)
+            nc.vector.tensor_tensor(
+                out=y[:, planes, halves[h]], in0=sums[:], in1=carried[:, planes, halves[h]], op=ALU.subtract
+            )
+
+        weave(nc.vector.tensor_copy, table_woven[0][:], table[:, :, halves[0]])
+        early_values = value_operands(0, ("val_picked0", "val_picked1"), f"larger{len(blocks) - 1}")
+        quantize(nc, table_codes[:, halves[0]], table_scales[:, halves[0]], table_woven[0][:])
+        weave(nc.vector.tensor_copy, table_woven[1][:], table[:, :, halves[1]])
+        left = values_times_table(0, 0, *early_values)
+        times_mem(0, 0, left)
+        quantize(nc, table_codes[:, halves[1]], table_scales[:, halves[1]], table_woven[1][:])
+        right = values_times_table(0, 1, *early_values)
+        less_carried(0, 0, left)
+        times_mem(0, 1, right)
+        late_values = value_operands(1, ("val_picked2", "table_woven0"), "table_woven1")
+        less_carried(0, 1, right)
+        nc.sync.dma_start(out=out_v[:, 0:2, :], in_=y[:, 0:2, :])
+
+        late_sums = [values_times_table(1, h, *late_values) for h in range(2)]
+        for h in range(2):
+            times_mem(1, h, late_sums[h])
+        for h in range(2):
+            less_carried(1, h, late_sums[h])
+            nc.sync.dma_start(out=out_v[:, 2:PACK, halves[h]], in_=y[:, 2:PACK, halves[h]])
+
         y_codes = sb.tile([P, J], U32, name="y_codes", align_bytes=64)
         y_scales = sb.tile([P, J], U8, name="y_scales", align_bytes=64)
-        shared_weave(nc, y_woven, y, 160)
-        quantize(nc, y_codes[:], y_scales[:], y_woven[:])
-        nc.sync.dma_start(out=out_1[0].rearrange("p c t -> p (c t)").bitcast(I32), in_=y_codes[:].bitcast(I32))
+        words_v = out_1[0].rearrange("p c t -> p (c t)").bitcast(I32)
+        y_woven = [sb.tile([P, HALF, PACK], BF16, name=f"y_woven{h}", align_bytes=64) for h in range(2)]
+        weave(nc.scalar.copy, y_woven[0][:, :SCALAR_COLS, :], y[:, :, :SCALAR_COLS])
+        weave(nc.vector.tensor_copy, y_woven[0][:, SCALAR_COLS:, :], y[:, :, SCALAR_COLS:HALF])
+        weave(nc.vector.tensor_copy, y_woven[1][:], y[:, :, halves[1]])
+        for h in range(2):
+            quantize(nc, y_codes[:, halves[h]], y_scales[:, halves[h]], y_woven[h][:])
+            nc.sync.dma_start(out=words_v[:, halves[h]], in_=y_codes[:, halves[h]].bitcast(I32))
         for q in range(4):
             queue = nc.sync if q % 2 else nc.scalar
             queue.dma_start(

from contextlib import ExitStack

import concourse.mybir as mybir
from concourse.masks import make_identity

D, T, I, J, U, Z, E = 512, 2048, 512, 512, 1024, 1024, 512
FLOPS = 2 * D * I * U + 2 * D * I * J + 2 * I * E * J

F32 = mybir.dt.float32
BF16 = mybir.dt.bfloat16
I32 = mybir.dt.int32
U32 = mybir.dt.uint32
U16 = mybir.dt.uint16
U8 = mybir.dt.uint8
FP8X4 = mybir.dt.float8_e4m3fn_x4
FP4X4 = mybir.dt.float4_e2m1fn_x4
ALU = mybir.AluOpType
COPY = mybir.ActivationFunctionType.Copy

P = 128
PACK = 4
BANK = 512
HALF = J // 2
CHUNK = 256
SCALAR_CHUNKS = 2
SCALAR_COLS = 192


def weave(engine_copy, woven, planes):
    engine_copy(
        out=woven.rearrange("p (c i) t -> p c t i", i=4),
        in_=planes.rearrange("p t (c i) -> p c t i", i=4),
    )


def quantize(nc, codes, scales, woven):
    nc.vector.quantize_mx(out=codes.bitcast(FP8X4), scales=scales, in_=woven.rearrange("p c t -> p (c t)"))


def tile_attend_tab_wideandown_changes_pl_kernel(
    tc, keys_words, keys_scales, notes, users2, rowf, vals, mem, offs, offs2, offs3, out_0, out_1, out_2
):
    nc = tc.nc
    with ExitStack() as ctx:
        lists = ctx.enter_context(tc.tile_pool(name="lists", bufs=1))
        sb = ctx.enter_context(tc.tile_pool(name="sb", bufs=1))
        psum = ctx.enter_context(tc.psum_pool(name="psum", bufs=1))

        token_list = lists.tile([P, I // 16], U16, name="token_list")
        note_list = lists.tile([P, J // 16], U16, name="note_list")
        user_list = lists.tile([P, J // 16], U16, name="user_list")

        key_words = sb.tile([P, T], U16, name="key_words", align_bytes=256)
        key_scales = sb.tile([P, T], U8, name="key_scales", align_bytes=256)
        note_rows = [sb.tile([P, PACK, CHUNK], F32, name=f"note_rows{c}", align_bytes=256) for c in range(U // CHUNK)]
        user_rows = [sb.tile([P, Z], F32, name=f"user_rows{t}", align_bytes=256) for t in range(PACK)]
        val_rows = [
            sb.tile([P, T], F32, name=f"val_rows{t}", tag=f"val_rows{t}", align_bytes=256) for t in range(PACK)
        ]
        row_factor = sb.tile([P, PACK], F32, name="row_factor")
        mem_cols = sb.tile([P, PACK], F32, name="mem_cols")

        nc.gpsimd.memset(key_scales[:].bitcast(I32), 0)
        notes_v = notes.rearrange("(p t) u -> p t u", t=PACK)
        users_v = users2.rearrange("(p t) z -> p t z", t=PACK)
        vals_v = vals.rearrange("(p t) c -> p t c", t=PACK)
        nc.sync.dma_start(out=key_words[:].bitcast(I32), in_=keys_words[0].bitcast(I32))
        nc.sync.dma_start(token_list[:], offs)
        for q in range(4):
            nc.sync.dma_start(
                out=key_scales[32 * q : 32 * q + 4, :].bitcast(I32),
                in_=keys_scales[0, 4 * q : 4 * q + 4, :].bitcast(I32),
            )
        for c in range(U // CHUNK):
            nc.sync.dma_start(out=note_rows[c][:], in_=notes_v[:, :, c * CHUNK : (c + 1) * CHUNK])
            if c == 1:
                nc.sync.dma_start(out=mem_cols[:], in_=mem.rearrange("o (p c) -> p (o c)", c=PACK))
        nc.sync.dma_start(user_list[:], offs3)
        nc.sync.dma_start(note_list[:], offs2)
        nc.sync.dma_start(out=row_factor[:], in_=rowf.rearrange("(p t) o -> p (t o)", t=PACK))
        for t in range(PACK):
            nc.sync.dma_start(out=user_rows[t][:], in_=users_v[:, t, :])
        for t in range(PACK):
            nc.sync.dma_start(out=val_rows[t][:], in_=vals_v[:, t, :])

        ident = sb.tile([P, P], F32, name="ident")
        make_identity(nc, ident[:])

        carried = sb.tile([P, PACK, J], F32, name="carried")
        nc.vector.memset(carried[:, :, 0:1], 0.0)

        picked_words = sb.tile([P, I], U16, name="picked_words")
        dealt_words = sb.tile([P, I], U16, name="dealt_words", align_bytes=64)
        dealt_scales = sb.tile([P, I], U8, name="dealt_scales", align_bytes=64)
        nc.vector.tensor_copy(picked_words[:], key_words[:].indirect(token_list[:]))
        nc.vector.tensor_copy(
            dealt_scales[:].rearrange("p (r s) -> p s r", r=PACK), key_scales[:].indirect(token_list[:])
        )
        nc.vector.tensor_copy(
            out=dealt_words[:].rearrange("p (r s) -> p r s", r=PACK),
            in_=picked_words[:].rearrange("p (s r) -> p r s", r=PACK),
        )

        def keys_times(bank, r, codes, scales):
            cols = slice(r * P, (r + 1) * P)
            nc.tensor.matmul_mx(
                out=bank,
                lhsT=dealt_words[:, cols].bitcast(FP4X4),
                lhsT_scale=dealt_scales[:, cols],
                rhs=codes.bitcast(FP8X4),
                rhs_scale=scales,
                start=True,
                stop=True,
            )

        note_woven = [
            sb.tile([P, CHUNK, PACK], BF16, name=f"note_woven{c}", align_bytes=64) for c in range(U // CHUNK)
        ]
        for c in range(SCALAR_CHUNKS):
            weave(nc.scalar.copy, note_woven[c][:], note_rows[c][:])

        mem_turned = psum.tile([P, PACK, P], F32, name="mem_turned", tag="narrow0")
        for c in range(PACK):
            nc.tensor.transpose(mem_turned[:, c, :], mem_cols[:, c : c + 1].to_broadcast([P, P]), ident[:])
        mem_row = sb.tile([P, J], F32, name="mem_row")
        nc.scalar.copy(
            out=mem_row[:].rearrange("p (k c) -> p k c", c=PACK), in_=mem_turned[:].rearrange("p c k -> p k c")
        )

        wide = sb.tile([P, PACK, U], F32, name="wide")
        for c in range(U // CHUNK):
            note_codes = sb.tile([P, CHUNK], U32, name=f"note_codes{c}", align_bytes=64)
            note_scales = sb.tile([P, CHUNK], U8, name=f"note_scales{c}", align_bytes=64)
            if c >= SCALAR_CHUNKS:
                weave(nc.vector.tensor_copy, note_woven[c][:], note_rows[c][:])
            quantize(nc, note_codes[:], note_scales[:], note_woven[c][:])
            for pair in range(2):
                bank = psum.tile([P, 2, CHUNK], F32, name="wide_bank", tag=f"main{(2 * c + pair) % 4}")
                for k in range(2):
                    keys_times(bank[:, k, :], 2 * pair + k, note_codes[:], note_scales[:])
                nc.scalar.copy(out=wide[:, 2 * pair : 2 * pair + 2, c * CHUNK : (c + 1) * CHUNK], in_=bank[:])

        halves = [slice(h * HALF, (h + 1) * HALF) for h in range(2)]
        list_halves = [slice(h * HALF // 16, (h + 1) * HALF // 16) for h in range(2)]
        last = PACK - 1
        wide_picked = [sb.tile([P, 2, J], F32, name=f"wide_picked{pair}") for pair in range(2)]
        for r in range(PACK):
            nc.scalar.activation(wide_picked[r // 2][:, r % 2, :], wide[:, r, :].indirect(note_list[:]), COPY)

        user_picked = sb.tile([P, PACK, J], BF16, name="user_picked")
        for t in range(last):
            nc.vector.tensor_copy(user_picked[:, t, :], user_rows[t][:].indirect(user_list[:]))
        for h in range(2):
            nc.vector.tensor_copy(
                user_picked[:, last, halves[h]], user_rows[last][:].indirect(user_list[:, list_halves[h]])
            )
        user_woven = [sb.tile([P, HALF, PACK], BF16, name=f"user_woven{h}", align_bytes=64) for h in range(2)]
        user_codes = [sb.tile([P, HALF], U32, name=f"user_codes{h}", align_bytes=64) for h in range(2)]
        user_scales = [sb.tile([P, HALF], U8, name=f"user_scales{h}", align_bytes=64) for h in range(2)]
        for h in range(2):
            weave(nc.vector.tensor_copy, user_woven[h][:], user_picked[:, :, halves[h]])
        for h in range(2):
            quantize(nc, user_codes[h][:], user_scales[h][:], user_woven[h][:])

        table = sb.tile([P, PACK, J], BF16, name="table")
        blocks = [(pair, h) for pair in range(2) for h in range(2)]
        larger = [
            sb.tile([P, 2, HALF], F32, name=f"larger{b}", tag=f"larger{b}", align_bytes=64) for b in range(len(blocks))
        ]

        def take_larger(b):
            pair, h = blocks[b]
            narrow = psum.tile([P, 2, HALF], F32, name="narrow", tag=f"narrow{b}")
            for k in range(2):
                keys_times(narrow[:, k, :], 2 * pair + k, user_codes[h][:], user_scales[h][:])
            nc.vector.tensor_tensor(out=larger[b][:], in0=narrow[:], in1=wide_picked[pair][:, :, halves[h]], op=ALU.max)

        def scale_rows(b):
            pair, h = blocks[b]
            for k in range(2):
                r = 2 * pair + k
                nc.vector.tensor_scalar(
                    out=table[:, r, halves[h]],
                    in0=larger[b][:, k, :],
                    scalar1=row_factor[:, r : r + 1],
                    scalar2=None,
                    op0=ALU.mult,
                )

        take_larger(0)
        for b in range(1, len(blocks)):
            take_larger(b)
            scale_rows(b - 1)
        scale_rows(len(blocks) - 1)

        table_woven = [
            sb.tile([P, HALF, PACK], BF16, name=f"table_woven{h}", tag=f"table_woven{h}", align_bytes=64)
            for h in range(2)
        ]
        table_codes = sb.tile([P, J], U32, name="table_codes", align_bytes=64)
        table_scales = sb.tile([P, J], U8, name="table_scales", align_bytes=64)

        def turn_values(t, picked_tag):
            val_picked = sb.tile([P, I], BF16, name=f"val_picked{t}", tag=picked_tag, align_bytes=64)
            nc.scalar.activation(val_picked[:], val_rows[t][:].indirect(token_list[:]), COPY)
            pairs = val_picked[:].bitcast(F32)
            turned = psum.tile([P, 2, P], F32, name="turned", tag=f"main{t}")
            for u in range(2):
                nc.tensor.transpose(turned[:, u, :], pairs[:, u : I // 2 : 2], ident[:])
            return turned[:].rearrange("p u e -> p e u")

        def value_operands(pair, picked_tags, codes_tag):
            turned = [turn_values(2 * pair + k, picked_tags[k]) for k in range(2)]
            woven = sb.tile(
                [P, 2 * P, PACK], BF16, name=f"val_woven{pair}", tag=f"val_rows{2 * pair + 1}", align_bytes=256
            )
            codes = sb.tile([P, 2 * P], U32, name=f"val_codes{pair}", tag=codes_tag, align_bytes=64)
            scales = sb.tile([P, 2 * P], U8, name=f"val_scales{pair}", align_bytes=64)
            for k in range(2):
                nc.scalar.copy(out=woven[:, k * P : (k + 1) * P, :].bitcast(F32), in_=turned[k])
            quantize(nc, codes[:], scales[:], woven[:])
            return codes, scales

        def values_times_table(pair, h, codes, scales):
            sums = psum.tile([P, 2, HALF], F32, name="sums", tag=f"narrow{2 * pair + h}")
            for k in range(2):
                plane = slice(k * P, (k + 1) * P)
                nc.tensor.matmul_mx(
                    out=sums[:, k, :],
                    lhsT=codes[:, plane].bitcast(FP8X4),
                    lhsT_scale=scales[:, plane],
                    rhs=table_codes[:, halves[h]].bitcast(FP8X4),
                    rhs_scale=table_scales[:, halves[h]],
                    start=True,
                    stop=True,
                )
            return sums

        y = sb.tile([P, PACK, J], F32, name="y", align_bytes=256)
        out_v = out_0.rearrange("(p t) c -> p t c", t=PACK)

        def times_mem(pair, h, sums):
            first = h * HALF + 1
            width = min(HALF, J - first)
            nc.vector.tensor_tensor(
                out=carried[:, 2 * pair : 2 * pair + 2, first : first + width],
                in0=sums[:, :, 0:width],
                in1=mem_row[:, first : first + width].unsqueeze(1).to_broadcast([P, 2, width]),
                op=ALU.mult,
            )

        def less_carried(pair, h, sums):
            planes = slice(2 * pair, 2 * pair + 2)
            nc.vector.tensor_tensor(
                out=y[:, planes, halves[h]], in0=sums[:], in1=carried[:, planes, halves[h]], op=ALU.subtract
            )

        weave(nc.vector.tensor_copy, table_woven[0][:], table[:, :, halves[0]])
        early_values = value_operands(0, ("val_picked0", "val_picked1"), f"larger{len(blocks) - 1}")
        quantize(nc, table_codes[:, halves[0]], table_scales[:, halves[0]], table_woven[0][:])
        weave(nc.vector.tensor_copy, table_woven[1][:], table[:, :, halves[1]])
        left = values_times_table(0, 0, *early_values)
        times_mem(0, 0, left)
        quantize(nc, table_codes[:, halves[1]], table_scales[:, halves[1]], table_woven[1][:])
        right = values_times_table(0, 1, *early_values)
        less_carried(0, 0, left)
        times_mem(0, 1, right)
        late_values = value_operands(1, ("val_picked2", "table_woven0"), "table_woven1")
        less_carried(0, 1, right)
        nc.sync.dma_start(out=out_v[:, 0:2, :], in_=y[:, 0:2, :])

        late_sums = [values_times_table(1, h, *late_values) for h in range(2)]
        for h in range(2):
            times_mem(1, h, late_sums[h])
        for h in range(2):
            less_carried(1, h, late_sums[h])
            nc.sync.dma_start(out=out_v[:, 2:PACK, halves[h]], in_=y[:, 2:PACK, halves[h]])

        y_codes = sb.tile([P, J], U32, name="y_codes", align_bytes=64)
        y_scales = sb.tile([P, J], U8, name="y_scales", align_bytes=64)
        words_v = out_1[0].rearrange("p c t -> p (c t)").bitcast(I32)
        y_woven = [sb.tile([P, HALF, PACK], BF16, name=f"y_woven{h}", align_bytes=64) for h in range(2)]
        weave(nc.scalar.copy, y_woven[0][:, :SCALAR_COLS, :], y[:, :, :SCALAR_COLS])
        weave(nc.vector.tensor_copy, y_woven[0][:, SCALAR_COLS:, :], y[:, :, SCALAR_COLS:HALF])
        weave(nc.vector.tensor_copy, y_woven[1][:], y[:, :, halves[1]])
        for h in range(2):
            quantize(nc, y_codes[:, halves[h]], y_scales[:, halves[h]], y_woven[h][:])
            nc.sync.dma_start(out=words_v[:, halves[h]], in_=y_codes[:, halves[h]].bitcast(I32))
        for q in range(4):
            queue = nc.sync if q % 2 else nc.scalar
            queue.dma_start(
                out=out_2[0, 4 * q : 4 * q + 4, :].bitcast(I32), in_=y_scales[32 * q : 32 * q + 4, :].bitcast(I32)
            )
